import numpy as np
import ml_dtypes


def mxq(x, axis, fmt="e4m3"):
    dtype, down = {"e4m3": (ml_dtypes.float8_e4m3fn, 7), "e5m2": (ml_dtypes.float8_e5m2, 14)}[fmt]
    v = np.moveaxis(np.asarray(x, np.float32).astype(ml_dtypes.bfloat16).astype(np.float64), axis, -1)
    blocks = v.reshape(v.shape[:-1] + (-1, 32))
    amax = np.abs(blocks).max(-1, keepdims=True)
    byte = np.maximum(np.where(amax > 0, np.frexp(amax)[1] - 1 + 127, 0) - down, 1)
    scale = np.exp2(byte - 127.0)
    codes = (blocks / scale).astype(np.float32).astype(dtype).astype(np.float64)
    return np.moveaxis((codes * scale).reshape(v.shape), -1, axis)


WIDE = False


def mx_kscale(k):
    if not WIDE:
        return np.ones(k)
    levels = np.array([10, -10, 5, -5, 0])
    if k % 512:
        return np.exp2(np.random.permutation(np.resize(levels, k // 32))).repeat(32)
    a = np.empty((k // 512, 16))
    for p in range(k // 512):
        a[p, :8] = np.random.permutation(np.resize(levels, 8))
        for g in range(8):
            far = levels[np.abs(levels - a[p, g]) >= 10]
            a[p, g + 8] = far[np.random.randint(len(far))]
    return np.exp2(a.ravel()).repeat(32)


BF16 = ml_dtypes.bfloat16


def bf(x):
    return np.asarray(x, np.float32).astype(BF16)


def f64(x):
    return np.asarray(x).astype(np.float64)


E2M1 = np.array([0.0, 0.5, 1.0, 1.5, 2.0, 3.0, 4.0, 6.0, -0.0, -0.5, -1.0, -1.5, -2.0, -3.0, -4.0, -6.0])


def pack_weight(w, fmt):
    k, n = w.shape
    w = f64(bf(w)).reshape(k // 32, 32, n)
    amax = np.abs(w).max(1)
    if fmt == "e4m3":
        byte = np.frexp(amax)[1] - 1 + 127 - 7
    else:
        mant, ex = np.frexp(amax / 6.0)
        byte = np.where(mant > 0.5, ex, ex - 1) + 127
    byte = np.clip(np.where(amax > 0, byte, 1), 1, 254)
    scaled = (w * np.exp2(127.0 - byte)[:, None, :]).reshape(k, n).astype(np.float32)
    by_word = np.ascontiguousarray(scaled.reshape(k // 512, 128, 4, n).transpose(0, 1, 3, 2))
    if fmt == "e4m3":
        words = by_word.astype(ml_dtypes.float8_e4m3fn).view(np.uint8)
    else:
        c = by_word.astype(ml_dtypes.float4_e2m1fn).view(np.uint8) & 0xF
        words = c[..., 0::2] | (c[..., 1::2] << 4)
    return np.ascontiguousarray(words), np.ascontiguousarray(byte.astype(np.uint8).reshape(k // 512, 16, n))


def unpack_weight(words, scales, fmt):
    g, p, n, _ = words.shape
    if fmt == "e4m3":
        vals = np.ascontiguousarray(words).view(ml_dtypes.float8_e4m3fn).astype(np.float64)
    else:
        nib = np.empty((g, p, n, 4), np.uint8)
        nib[..., 0::2] = words & 0xF
        nib[..., 1::2] = words >> 4
        vals = E2M1[nib]
    vals = vals * np.repeat(np.exp2(scales.astype(np.float64) - 127.0), 8, axis=1)[..., None]
    return vals.transpose(0, 1, 3, 2).reshape(g * 512, n)
def pack4(w):
    words, scales = pack_weight(w, "e2m1")
    return words.reshape(words.shape[0], 128, -1), scales


def unpack4(words, scales):
    return unpack_weight(words.reshape(words.shape[0], 128, -1, 2), scales, "e2m1")


T, R, E = 1536, 2560, 1024


def setup_inputs():
    s = mx_kscale(T)
    t = mx_kscale(R)
    z = 2 * np.random.standard_normal((T + R, E)) - 1
    logged = 1 / (1 + np.exp(-(z[T:] + np.random.standard_normal((R, E)))))
    h_words, h_scales = pack4(logged / t[:, None])
    credit = 4 * np.random.standard_normal(T + R) / np.sqrt(T + R)
    return {"z": bf(z),
            "credit": bf(credit * np.concatenate([s, t])),
            "trust": bf((1 + 0.1 * np.random.standard_normal(T)) / s),
            "h_words": h_words,
            "h_scales": h_scales}


def reference(z, credit, trust, h_words, h_scales):
    g = 1 / (1 + np.exp(-f64(z)))
    left = g * f64(credit)[:, None]
    right = g[:T] * f64(trust)[:, None]
    fresh_left = mxq(left[:T], 0, "e4m3")
    fresh_right = mxq(right, 0, "e4m3")
    replay_left = mxq(left[T:], 0, "e4m3")
    h = unpack4(h_words, h_scales)
    return (fresh_left.T @ fresh_right) + (replay_left.T @ h)

@@ -1,0 +1,240 @@
+from contextlib import ExitStack
+
+import concourse.mybir as mybir
+from concourse.masks import make_identity
+
+T, R, E = 1536, 2560, 1024
+FLOPS = 2 * (T + R) * E * E
+
+F32 = mybir.dt.float32
+BF16 = mybir.dt.bfloat16
+I32 = mybir.dt.int32
+U32 = mybir.dt.uint32
+U8 = mybir.dt.uint8
+FP8X4 = mybir.dt.float8_e4m3fn_x4
+FP4X4 = mybir.dt.float4_e2m1fn_x4
+MULT = mybir.AluOpType.mult
+SIGMOID = mybir.ActivationFunctionType.Sigmoid
+
+P = 128
+PACK = 4
+K_PASS = P * PACK
+FRESH = T // K_PASS
+REPLAY = R // K_PASS
+PASSES = FRESH + REPLAY
+UNIT = 256
+HALF = 512
+M_TILE = 128
+ACC_BANKS = 7
+GATE_SLOTS = 18
+AHEAD = 2
+POOL_COLS = 224
+OUT_BUFS = 4
+
+
+def plan_steps():
+    def right(g, h):
+        return [("V", g, 2 * h), ("V", g, 2 * h + 1)]
+
+    def fresh(j):
+        return [("L", g, j) for g in range(FRESH)]
+
+    def replay(j):
+        return [("L", g, j) for g in range(FRESH, PASSES)]
+
+    f0, f1, r0, r1 = fresh(0), fresh(1), replay(0), replay(1)
+    order = []
+    for g in range(FRESH):
+        order = order + right(g, 0) + [f0[g]]
+    order = order + r0 + [r1[0]]
+    order = order + right(0, 1) + [r1[1]]
+    order = order + [r1[2], r1[3], f1[0]]
+    order = order + right(1, 1) + [f1[1]]
+    order = order + right(2, 1) + [r1[4]]
+    order = order + [f1[2]]
+    for j in (2, 3):
+        order = order + replay(j) + fresh(j)
+    return [order[i : i + 3] for i in range(0, len(order), 3)]
+
+
+def tile_router_gate_coactivation_s1_kernel(tc, z, credit, trust, h_words, h_scales, out):
+    nc = tc.nc
+    steps = plan_steps()
+
+    with ExitStack() as ctx:
+        keep = ctx.enter_context(tc.tile_pool(name="keep", bufs=1))
+        stage = ctx.enter_context(tc.tile_pool(name="stage", bufs=2))
+        outp = ctx.enter_context(tc.tile_pool(name="outp", bufs=OUT_BUFS))
+        psum = ctx.enter_context(tc.psum_pool(name="psum", bufs=1))
+        ctx.enter_context(tc.manual_schedule())
+
+        w_rows = keep.tile([PASSES + FRESH, K_PASS], BF16, name="w_rows")
+        nc.sync.dma_start(out=w_rows[0:PASSES, :], in_=credit.rearrange("(g k) -> g k", k=K_PASS))
+        nc.sync.dma_start(out=w_rows[PASSES : PASSES + FRESH, :], in_=trust.rearrange("(g k) -> g k", k=K_PASS))
+
+        z_tiles = {}
+
+        def load_z(g, c0, width):
+            zt = keep.tile([P, PACK, width], BF16, name="z_%d_%d" % (g, c0))
+            rows = z[g * K_PASS : (g + 1) * K_PASS, c0 : c0 + width]
+            nc.sync.dma_start(out=zt[:], in_=rows.rearrange("(p t) n -> p t n", t=PACK))
+            for c in range(c0, c0 + width, UNIT):
+                z_tiles[(g, c // UNIT)] = zt[:, :, c - c0 : c - c0 + UNIT]
+
+        h_tiles = {}
+
+        def load_h(g0, g1):
+            ht = keep.tile([P, g1 - g0, 2 * E], U8, name="h_%d" % g0, align_bytes=64)
+            nc.sync.dma_start(out=ht[:].bitcast(I32), in_=h_words[g0:g1].rearrange("g p w -> p g w").bitcast(I32))
+            for g in range(g0, g1):
+                h_tiles[g] = ht[:, g - g0, :]
+
+        ident = keep.tile([P, P], F32, name="ident")
+        make_identity(nc, ident[:])
+        h_plane = keep.tile([P, REPLAY, E], U8, name="h_plane", align_bytes=64)
+        nc.gpsimd.memset(h_plane[:].bitcast(I32), 0)
+        w_slots = keep.tile([P, PACK, P], F32, name="w_slots")
+        nc.vector.memset(w_slots[:], 0.0)
+
+        load_z(0, 0, UNIT)
+        load_z(0, UNIT, UNIT)
+        for g in range(1, FRESH + 3):
+            load_z(g, 0, HALF)
+        for q in range(4):
+            nc.sync.dma_start(
+                out=h_plane[32 * q : 32 * q + 4].bitcast(I32),
+                in_=h_scales[:, 4 * q : 4 * q + 4, :].rearrange("g r n -> r g n").bitcast(I32),
+            )
+        load_h(0, 3)
+        for g in range(FRESH + 3, PASSES):
+            load_z(g, 0, HALF)
+        load_h(3, REPLAY)
+        for g in range(PASSES):
+            load_z(g, HALF, HALF)
+
+        nc.vector.tensor_copy(
+            out=w_slots[0 : PASSES + FRESH], in_=w_rows[:].rearrange("r (p t) -> r t p", t=PACK)
+        )
+        w_psum = psum.tile([P, P, PACK], F32, name="w_psum")
+        for t in range(PACK):
+            nc.tensor.transpose(w_psum[:, :, t], w_slots[:, t, :], ident[:])
+        w_sbuf = keep.tile([P, PASSES + FRESH, PACK], F32, name="w_sbuf")
+        nc.vector.tensor_copy(out=w_sbuf[:], in_=w_psum[:, 0 : PASSES + FRESH, :])
+
+        last_use = {}
+        for s, step in enumerate(steps):
+            for side, g, j in step:
+                last_use[(g, j)] = s
+        gates = {}
+        free_slots = list(range(GATE_SLOTS))
+        slot_of = {}
+
+        def sigmoid(g, j):
+            slot = free_slots.pop(0)
+            slot_of[(g, j)] = slot
+            gt = keep.tile([P, PACK, UNIT], F32, name="gate", tag="gate%d" % slot)
+            nc.scalar.activation(out=gt[:], in_=z_tiles[(g, j)], func=SIGMOID)
+            gates[(g, j)] = gt
+
+        def weigh(engine, weights, unit, dst, c0, c1):
+            side, g, j = unit
+            row = g if side == "L" else PASSES + g
+            pairs = (c1 - c0) // 2
+            engine.tensor_tensor(
+                out=dst[:, PACK * c0 : PACK * c1].rearrange("p (c i t) -> p c t i", i=2, t=PACK),
+                in0=gates[(g, j)][:, :, c0:c1].rearrange("p t (c i) -> p c t i", i=2),
+                in1=weights[:, row, :].unsqueeze(1).unsqueeze(3).to_broadcast([P, pairs, PACK, 2]),
+                op=MULT,
+            )
+
+        coded = {}
+
+        def quantize(units, src, name):
+            width = UNIT * len(units)
+            codes = keep.tile([P, width], U32, name="codes_" + name, align_bytes=64)
+            scales = keep.tile([P, width], U8, name="scales_" + name, align_bytes=64)
+            nc.vector.quantize_mx(out=codes[:].bitcast(FP8X4), scales=scales[:], in_=src)
+            for i, unit in enumerate(units):
+                coded[unit] = (codes, scales, i * UNIT)
+
+        todo = {(m, h): list(range(PASSES)) for m in range(E // M_TILE) for h in range(E // HALF)}
+        banks = {}
+        free_banks = list(range(ACC_BANKS))
+        closed = []
+
+        def ready(m, h, g):
+            left = ("L", g, m * M_TILE // UNIT) in coded
+            return left and (g >= FRESH or ("V", g, 2 * h) in coded)
+
+        def multiply():
+            for h, m in [(h, m) for j in range(E // UNIT) for h in range(2) for m in (2 * j, 2 * j + 1)]:
+                now = [g for g in todo[(m, h)] if ready(m, h, g)]
+                if now and (m, h) not in banks and free_banks:
+                    b = free_banks.pop(0)
+                    banks[(m, h)] = (b, psum.tile([P, HALF], F32, name="acc", tag="acc%d" % b))
+                if not now or (m, h) not in banks:
+                    continue
+                acc = banks[(m, h)][1]
+                for g in now:
+                    first = len(todo[(m, h)]) == PASSES
+                    todo[(m, h)].remove(g)
+                    last = not todo[(m, h)]
+                    codes, scales, c0 = coded[("L", g, m * M_TILE // UNIT)]
+                    c0 = c0 + (m * M_TILE) % UNIT
+                    if g < FRESH:
+                        v_codes, v_scales, v0 = coded[("V", g, 2 * h)]
+                        rhs, rhs_scale = v_codes[:].bitcast(FP8X4), v_scales[:]
+                    else:
+                        rhs = h_tiles[g - FRESH][:, 2 * HALF * h : 2 * HALF * (h + 1)].bitcast(FP4X4)
+                        rhs_scale = h_plane[:, g - FRESH, HALF * h : HALF * (h + 1)]
+                    nc.tensor.matmul_mx(
+                        out=acc[:],
+                        lhsT=codes[:, c0 : c0 + M_TILE].bitcast(FP8X4),
+                        lhsT_scale=scales[:, c0 : c0 + M_TILE],
+                        rhs=rhs,
+                        rhs_scale=rhs_scale,
+                        start=first,
+                        stop=last,
+                    )
+                    if last:
+                        closed.append((m, h))
+
+        def drain(share):
+            for i, (m, h) in enumerate(list(closed)):
+                closed.remove((m, h))
+                b, acc = banks[(m, h)]
+                res = outp.tile([P, HALF], F32, name="res")
+                if share and i % 2 == 1:
+                    nc.vector.tensor_copy(out=res[:], in_=acc[:])
+                else:
+                    nc.scalar.copy(out=res[:], in_=acc[:])
+                nc.sync.dma_start(out=out[m * M_TILE : (m + 1) * M_TILE, h * HALF : (h + 1) * HALF], in_=res[:])
+                free_banks.append(b)
+
+        for s, step in enumerate(steps):
+            for later in steps[s : s + AHEAD + 1]:
+                for side, g, j in later:
+                    if (g, j) not in gates:
+                        sigmoid(g, j)
+            pair = stage.tile([P, 2 * UNIT * PACK], BF16, name="pair", align_bytes=64)
+            weigh(nc.vector, w_psum, step[0], pair[:, 0 : UNIT * PACK], 0, UNIT)
+            if len(step) == 3:
+                single = stage.tile([P, UNIT * PACK], BF16, name="single", align_bytes=64, bufs=1)
+                weigh(nc.gpsimd, w_sbuf, step[2], single, 0, POOL_COLS)
+                weigh(nc.vector, w_psum, step[2], single, POOL_COLS, UNIT)
+            weigh(nc.vector, w_psum, step[1], pair[:, UNIT * PACK : 2 * UNIT * PACK], 0, UNIT)
+            if len(step) == 3:
+                quantize(step[0:2], pair[:], "pair%d" % s)
+                quantize(step[2:3], single[:], "single%d" % s)
+            else:
+                quantize(step[0:1], pair[:, 0 : UNIT * PACK], "a%d" % s)
+                quantize(step[1:2], pair[:, UNIT * PACK : 2 * UNIT * PACK], "b%d" % s)
+            for side, g, j in step:
+                if last_use[(g, j)] == s and (g, j) in slot_of:
+                    free_slots.append(slot_of.pop((g, j)))
+            drain(False)
+            multiply()
+        drain(True)
+        multiply()
+        drain(True)
+        assert not any(todo.values())

@@ -28,7 +28,7 @@ M_TILE = 128
 ACC_BANKS = 7
 GATE_SLOTS = 18
 AHEAD = 2
-POOL_COLS = 224
+POOL_COLS = 176
 OUT_BUFS = 4
 
 
@@ -68,9 +68,8 @@ def tile_router_gate_coactivation_s1_kernel(tc, z, credit, trust, h_words, h_sca
         psum = ctx.enter_context(tc.psum_pool(name="psum", bufs=1))
         ctx.enter_context(tc.manual_schedule())
 
-        w_rows = keep.tile([PASSES + FRESH, K_PASS], BF16, name="w_rows")
-        nc.sync.dma_start(out=w_rows[0:PASSES, :], in_=credit.rearrange("(g k) -> g k", k=K_PASS))
-        nc.sync.dma_start(out=w_rows[PASSES : PASSES + FRESH, :], in_=trust.rearrange("(g k) -> g k", k=K_PASS))
+        w_rows = keep.tile([P, K_PASS], BF16, name="w_rows")
+        nc.gpsimd.memset(w_rows[:], 0.0)
 
         z_tiles = {}
 
@@ -93,10 +92,10 @@ def tile_router_gate_coactivation_s1_kernel(tc, z, credit, trust, h_words, h_sca
         make_identity(nc, ident[:])
         h_plane = keep.tile([P, REPLAY, E], U8, name="h_plane", align_bytes=64)
         nc.gpsimd.memset(h_plane[:].bitcast(I32), 0)
-        w_slots = keep.tile([P, PACK, P], F32, name="w_slots")
-        nc.vector.memset(w_slots[:], 0.0)
 
         load_z(0, 0, UNIT)
+        nc.sync.dma_start(out=w_rows[0:PASSES, :], in_=credit.rearrange("(g k) -> g k", k=K_PASS))
+        nc.sync.dma_start(out=w_rows[PASSES : PASSES + FRESH, :], in_=trust.rearrange("(g k) -> g k", k=K_PASS))
         load_z(0, UNIT, UNIT)
         for g in range(1, FRESH + 3):
             load_z(g, 0, HALF)
@@ -112,12 +111,11 @@ def tile_router_gate_coactivation_s1_kernel(tc, z, credit, trust, h_words, h_sca
         for g in range(PASSES):
             load_z(g, HALF, HALF)
 
-        nc.vector.tensor_copy(
-            out=w_slots[0 : PASSES + FRESH], in_=w_rows[:].rearrange("r (p t) -> r t p", t=PACK)
-        )
-        w_psum = psum.tile([P, P, PACK], F32, name="w_psum")
-        for t in range(PACK):
-            nc.tensor.transpose(w_psum[:, :, t], w_slots[:, t, :], ident[:])
+        w_bank = psum.tile([P, P, 2], F32, name="w_bank")
+        w_words = w_rows[:].bitcast(F32)
+        for u in range(2):
+            nc.tensor.transpose(w_bank[:, :, u], w_words[:, u : K_PASS // 2 : 2], ident[:])
+        w_psum = w_bank[:].rearrange("p j u -> p (j u)").bitcast(BF16).rearrange("p (j t) -> p j t", t=PACK)
         w_sbuf = keep.tile([P, PASSES + FRESH, PACK], F32, name="w_sbuf")
         nc.vector.tensor_copy(out=w_sbuf[:], in_=w_psum[:, 0 : PASSES + FRESH, :])
 
@@ -224,8 +222,8 @@ def tile_router_gate_coactivation_s1_kernel(tc, z, credit, trust, h_words, h_sca
                 weigh(nc.vector, w_psum, step[2], single, POOL_COLS, UNIT)
             weigh(nc.vector, w_psum, step[1], pair[:, UNIT * PACK : 2 * UNIT * PACK], 0, UNIT)
             if len(step) == 3:
-                quantize(step[0:2], pair[:], "pair%d" % s)
                 quantize(step[2:3], single[:], "single%d" % s)
+                quantize(step[0:2], pair[:], "pair%d" % s)
             else:
                 quantize(step[0:1], pair[:, 0 : UNIT * PACK], "a%d" % s)
                 quantize(step[1:2], pair[:, UNIT * PACK : 2 * UNIT * PACK], "b%d" % s)

@@ -28,7 +28,7 @@ M_TILE = 128
 ACC_BANKS = 7
 GATE_SLOTS = 18
 AHEAD = 2
-POOL_COLS = 176
+POOL_COLS = 200
 OUT_BUFS = 4
 
 
@@ -46,11 +46,10 @@ def plan_steps():
     order = []
     for g in range(FRESH):
         order = order + right(g, 0) + [f0[g]]
-    order = order + r0 + [r1[0]]
-    order = order + right(0, 1) + [r1[1]]
-    order = order + [r1[2], r1[3], f1[0]]
-    order = order + right(1, 1) + [f1[1]]
-    order = order + right(2, 1) + [r1[4]]
+    order = order + r0 + r1[0:4]
+    order = order + right(0, 1) + [r1[4]]
+    order = order + right(1, 1) + [f1[0]]
+    order = order + right(2, 1) + [f1[1]]
     order = order + [f1[2]]
     for j in (2, 3):
         order = order + replay(j) + fresh(j)
@@ -88,6 +87,13 @@ def tile_router_gate_coactivation_s1_kernel(tc, z, credit, trust, h_words, h_sca
             for g in range(g0, g1):
                 h_tiles[g] = ht[:, g - g0, :]
 
+        def load_scales():
+            for q in range(4):
+                nc.sync.dma_start(
+                    out=h_plane[32 * q : 32 * q + 4].bitcast(I32),
+                    in_=h_scales[:, 4 * q : 4 * q + 4, :].rearrange("g r n -> r g n").bitcast(I32),
+                )
+
         ident = keep.tile([P, P], F32, name="ident")
         make_identity(nc, ident[:])
         h_plane = keep.tile([P, REPLAY, E], U8, name="h_plane", align_bytes=64)
@@ -95,18 +101,14 @@ def tile_router_gate_coactivation_s1_kernel(tc, z, credit, trust, h_words, h_sca
 
         load_z(0, 0, UNIT)
         nc.sync.dma_start(out=w_rows[0:PASSES, :], in_=credit.rearrange("(g k) -> g k", k=K_PASS))
-        nc.sync.dma_start(out=w_rows[PASSES : PASSES + FRESH, :], in_=trust.rearrange("(g k) -> g k", k=K_PASS))
+        trust_rows = trust.rearrange("(g k) -> g k", k=K_PASS)
+        nc.sync.dma_start(out=w_rows[PASSES : PASSES + 2, :], in_=trust_rows[0:2])
+        nc.sync.dma_start(out=w_rows[PASSES + 2 : PASSES + FRESH, :], in_=trust_rows[2:FRESH])
         load_z(0, UNIT, UNIT)
-        for g in range(1, FRESH + 3):
+        for g in range(1, PASSES):
             load_z(g, 0, HALF)
-        for q in range(4):
-            nc.sync.dma_start(
-                out=h_plane[32 * q : 32 * q + 4].bitcast(I32),
-                in_=h_scales[:, 4 * q : 4 * q + 4, :].rearrange("g r n -> r g n").bitcast(I32),
-            )
+        load_scales()
         load_h(0, 3)
-        for g in range(FRESH + 3, PASSES):
-            load_z(g, 0, HALF)
         load_h(3, REPLAY)
         for g in range(PASSES):
             load_z(g, HALF, HALF)

@@ -28,7 +28,7 @@ M_TILE = 128
 ACC_BANKS = 7
 GATE_SLOTS = 18
 AHEAD = 2
-POOL_COLS = 200
+POOL_COLS = 216
 OUT_BUFS = 4
 
 
@@ -43,16 +43,9 @@ def plan_steps():
         return [("L", g, j) for g in range(FRESH, PASSES)]
 
     f0, f1, r0, r1 = fresh(0), fresh(1), replay(0), replay(1)
-    order = []
-    for g in range(FRESH):
-        order = order + right(g, 0) + [f0[g]]
-    order = order + r0 + r1[0:4]
-    order = order + right(0, 1) + [r1[4]]
-    order = order + right(1, 1) + [f1[0]]
-    order = order + right(2, 1) + [f1[1]]
-    order = order + [f1[2]]
-    for j in (2, 3):
-        order = order + replay(j) + fresh(j)
+    both = [unit for pair in zip(r0, r1) for unit in pair]
+    r2 = replay(2)
+    order = right(0, 0) + [f0[0]] + right(1, 0) + [f0[1]] + right(2, 0) + [f0[2]] + both[0:9] + right(0, 1) + [both[9]] + right(1, 1) + [f1[0]] + right(2, 1) + [f1[1]] + r2[0:2] + [f1[2]] + r2[2:5] + fresh(2) + replay(3) + fresh(3)
     return [order[i : i + 3] for i in range(0, len(order), 3)]
 
 
@@ -77,7 +70,8 @@ def tile_router_gate_coactivation_s1_kernel(tc, z, credit, trust, h_words, h_sca
             rows = z[g * K_PASS : (g + 1) * K_PASS, c0 : c0 + width]
             nc.sync.dma_start(out=zt[:], in_=rows.rearrange("(p t) n -> p t n", t=PACK))
             for c in range(c0, c0 + width, UNIT):
-                z_tiles[(g, c // UNIT)] = zt[:, :, c - c0 : c - c0 + UNIT]
+                w = min(width, UNIT)
+                z_tiles.setdefault((g, c // UNIT), []).append((c % UNIT, w, zt[:, :, c - c0 : c - c0 + w]))
 
         h_tiles = {}
 
@@ -105,13 +99,24 @@ def tile_router_gate_coactivation_s1_kernel(tc, z, credit, trust, h_words, h_sca
         nc.sync.dma_start(out=w_rows[PASSES : PASSES + 2, :], in_=trust_rows[0:2])
         nc.sync.dma_start(out=w_rows[PASSES + 2 : PASSES + FRESH, :], in_=trust_rows[2:FRESH])
         load_z(0, UNIT, UNIT)
-        for g in range(1, PASSES):
-            load_z(g, 0, HALF)
+        load_z(1, 0, HALF)
+        load_z(2, 0, HALF)
+        load_z(3, 0, HALF)
+        load_z(4, 0, HALF)
+        load_z(5, 0, HALF)
+        load_z(6, 0, HALF)
+        load_z(7, 0, HALF)
         load_scales()
-        load_h(0, 3)
-        load_h(3, REPLAY)
-        for g in range(PASSES):
-            load_z(g, HALF, HALF)
+        load_h(0, 2)
+        load_z(0, HALF, HALF)
+        load_h(2, REPLAY)
+        load_z(1, HALF, HALF)
+        load_z(2, HALF, HALF)
+        load_z(3, HALF, HALF)
+        load_z(4, HALF, HALF)
+        load_z(5, HALF, HALF)
+        load_z(6, HALF, HALF)
+        load_z(7, HALF, HALF)
 
         w_bank = psum.tile([P, P, 2], F32, name="w_bank")
         w_words = w_rows[:].bitcast(F32)
@@ -133,7 +138,8 @@ def tile_router_gate_coactivation_s1_kernel(tc, z, credit, trust, h_words, h_sca
             slot = free_slots.pop(0)
             slot_of[(g, j)] = slot
             gt = keep.tile([P, PACK, UNIT], F32, name="gate", tag="gate%d" % slot)
-            nc.scalar.activation(out=gt[:], in_=z_tiles[(g, j)], func=SIGMOID)
+            for c0, w, logits in z_tiles[(g, j)]:
+                nc.scalar.activation(out=gt[:, :, c0 : c0 + w], in_=logits, func=SIGMOID)
             gates[(g, j)] = gt
 
         def weigh(engine, weights, unit, dst, c0, c1):
@@ -225,6 +231,8 @@ def tile_router_gate_coactivation_s1_kernel(tc, z, credit, trust, h_words, h_sca
             weigh(nc.vector, w_psum, step[1], pair[:, UNIT * PACK : 2 * UNIT * PACK], 0, UNIT)
             if len(step) == 3:
                 quantize(step[2:3], single[:], "single%d" % s)
+                drain(False)
+                multiply()
                 quantize(step[0:2], pair[:], "pair%d" % s)
             else:
                 quantize(step[0:1], pair[:, 0 : UNIT * PACK], "a%d" % s)

@@ -22,14 +22,16 @@ K_PASS = P * PACK
 FRESH = T // K_PASS
 REPLAY = R // K_PASS
 PASSES = FRESH + REPLAY
+WEIGHT_ROWS = PASSES + FRESH
 UNIT = 256
 HALF = 512
 M_TILE = 128
 ACC_BANKS = 7
 GATE_SLOTS = 18
 AHEAD = 2
-POOL_COLS = 216
+POOL_COLS = 232
 OUT_BUFS = 4
+H_FIRST = 2
 
 
 def plan_steps():
@@ -42,10 +44,16 @@ def plan_steps():
     def replay(j):
         return [("L", g, j) for g in range(FRESH, PASSES)]
 
-    f0, f1, r0, r1 = fresh(0), fresh(1), replay(0), replay(1)
-    both = [unit for pair in zip(r0, r1) for unit in pair]
-    r2 = replay(2)
-    order = right(0, 0) + [f0[0]] + right(1, 0) + [f0[1]] + right(2, 0) + [f0[2]] + both[0:9] + right(0, 1) + [both[9]] + right(1, 1) + [f1[0]] + right(2, 1) + [f1[1]] + r2[0:2] + [f1[2]] + r2[2:5] + fresh(2) + replay(3) + fresh(3)
+    order = []
+    for g in range(FRESH):
+        order = order + right(g, 0) + [fresh(0)[g]]
+    replay_01 = [unit for both in zip(replay(0), replay(1)) for unit in both]
+    order = order + replay_01[:-1]
+    rest_of_1 = replay_01[-1:] + fresh(1)
+    for g in range(FRESH):
+        order = order + right(g, 1) + [rest_of_1[g]]
+    order = order + replay(2)[:2] + rest_of_1[FRESH:] + replay(2)[2:] + fresh(2)
+    order = order + replay(3) + fresh(3)
     return [order[i : i + 3] for i in range(0, len(order), 3)]
 
 
@@ -63,30 +71,21 @@ def tile_router_gate_coactivation_s1_kernel(tc, z, credit, trust, h_words, h_sca
         w_rows = keep.tile([P, K_PASS], BF16, name="w_rows")
         nc.gpsimd.memset(w_rows[:], 0.0)
 
-        z_tiles = {}
+        logits = {}
+        h_codes = {}
 
         def load_z(g, c0, width):
             zt = keep.tile([P, PACK, width], BF16, name="z_%d_%d" % (g, c0))
             rows = z[g * K_PASS : (g + 1) * K_PASS, c0 : c0 + width]
             nc.sync.dma_start(out=zt[:], in_=rows.rearrange("(p t) n -> p t n", t=PACK))
-            for c in range(c0, c0 + width, UNIT):
-                w = min(width, UNIT)
-                z_tiles.setdefault((g, c // UNIT), []).append((c % UNIT, w, zt[:, :, c - c0 : c - c0 + w]))
-
-        h_tiles = {}
+            for c in range(0, width, UNIT):
+                logits[(g, (c0 + c) // UNIT)] = zt[:, :, c : c + UNIT]
 
         def load_h(g0, g1):
             ht = keep.tile([P, g1 - g0, 2 * E], U8, name="h_%d" % g0, align_bytes=64)
             nc.sync.dma_start(out=ht[:].bitcast(I32), in_=h_words[g0:g1].rearrange("g p w -> p g w").bitcast(I32))
             for g in range(g0, g1):
-                h_tiles[g] = ht[:, g - g0, :]
-
-        def load_scales():
-            for q in range(4):
-                nc.sync.dma_start(
-                    out=h_plane[32 * q : 32 * q + 4].bitcast(I32),
-                    in_=h_scales[:, 4 * q : 4 * q + 4, :].rearrange("g r n -> r g n").bitcast(I32),
-                )
+                h_codes[g] = ht[:, g - g0, :]
 
         ident = keep.tile([P, P], F32, name="ident")
         make_identity(nc, ident[:])
@@ -97,59 +96,47 @@ def tile_router_gate_coactivation_s1_kernel(tc, z, credit, trust, h_words, h_sca
         nc.sync.dma_start(out=w_rows[0:PASSES, :], in_=credit.rearrange("(g k) -> g k", k=K_PASS))
         trust_rows = trust.rearrange("(g k) -> g k", k=K_PASS)
         nc.sync.dma_start(out=w_rows[PASSES : PASSES + 2, :], in_=trust_rows[0:2])
-        nc.sync.dma_start(out=w_rows[PASSES + 2 : PASSES + FRESH, :], in_=trust_rows[2:FRESH])
+        nc.sync.dma_start(out=w_rows[PASSES + 2 : WEIGHT_ROWS, :], in_=trust_rows[2:FRESH])
         load_z(0, UNIT, UNIT)
-        load_z(1, 0, HALF)
-        load_z(2, 0, HALF)
-        load_z(3, 0, HALF)
-        load_z(4, 0, HALF)
-        load_z(5, 0, HALF)
-        load_z(6, 0, HALF)
-        load_z(7, 0, HALF)
-        load_scales()
-        load_h(0, 2)
+        for g in range(1, PASSES):
+            load_z(g, 0, HALF)
+        for quadrant in range(4):
+            nc.sync.dma_start(
+                out=h_plane[32 * quadrant : 32 * quadrant + 4].bitcast(I32),
+                in_=h_scales[:, 4 * quadrant : 4 * quadrant + 4, :].rearrange("g r n -> r g n").bitcast(I32),
+            )
+        load_h(0, H_FIRST)
         load_z(0, HALF, HALF)
-        load_h(2, REPLAY)
-        load_z(1, HALF, HALF)
-        load_z(2, HALF, HALF)
-        load_z(3, HALF, HALF)
-        load_z(4, HALF, HALF)
-        load_z(5, HALF, HALF)
-        load_z(6, HALF, HALF)
-        load_z(7, HALF, HALF)
+        load_h(H_FIRST, REPLAY)
+        for g in range(1, PASSES):
+            load_z(g, HALF, HALF)
 
         w_bank = psum.tile([P, P, 2], F32, name="w_bank")
         w_words = w_rows[:].bitcast(F32)
         for u in range(2):
             nc.tensor.transpose(w_bank[:, :, u], w_words[:, u : K_PASS // 2 : 2], ident[:])
         w_psum = w_bank[:].rearrange("p j u -> p (j u)").bitcast(BF16).rearrange("p (j t) -> p j t", t=PACK)
-        w_sbuf = keep.tile([P, PASSES + FRESH, PACK], F32, name="w_sbuf")
-        nc.vector.tensor_copy(out=w_sbuf[:], in_=w_psum[:, 0 : PASSES + FRESH, :])
+        w_sbuf = keep.tile([P, WEIGHT_ROWS, PACK], F32, name="w_sbuf")
+        nc.vector.tensor_copy(out=w_sbuf[:], in_=w_psum[:, 0:WEIGHT_ROWS, :])
 
-        last_use = {}
-        for s, step in enumerate(steps):
-            for side, g, j in step:
-                last_use[(g, j)] = s
+        last_use = {(g, j): s for s, step in enumerate(steps) for side, g, j in step}
         gates = {}
         free_slots = list(range(GATE_SLOTS))
         slot_of = {}
 
         def sigmoid(g, j):
-            slot = free_slots.pop(0)
-            slot_of[(g, j)] = slot
-            gt = keep.tile([P, PACK, UNIT], F32, name="gate", tag="gate%d" % slot)
-            for c0, w, logits in z_tiles[(g, j)]:
-                nc.scalar.activation(out=gt[:, :, c0 : c0 + w], in_=logits, func=SIGMOID)
+            slot_of[(g, j)] = free_slots.pop(0)
+            gt = keep.tile([P, PACK, UNIT], F32, name="gate", tag="gate%d" % slot_of[(g, j)])
+            nc.scalar.activation(out=gt[:], in_=logits[(g, j)], func=SIGMOID)
             gates[(g, j)] = gt
 
         def weigh(engine, weights, unit, dst, c0, c1):
             side, g, j = unit
             row = g if side == "L" else PASSES + g
-            pairs = (c1 - c0) // 2
             engine.tensor_tensor(
                 out=dst[:, PACK * c0 : PACK * c1].rearrange("p (c i t) -> p c t i", i=2, t=PACK),
                 in0=gates[(g, j)][:, :, c0:c1].rearrange("p t (c i) -> p c t i", i=2),
-                in1=weights[:, row, :].unsqueeze(1).unsqueeze(3).to_broadcast([P, pairs, PACK, 2]),
+                in1=weights[:, row, :].unsqueeze(1).unsqueeze(3).to_broadcast([P, (c1 - c0) // 2, PACK, 2]),
                 op=MULT,
             )
 
@@ -163,40 +150,37 @@ def tile_router_gate_coactivation_s1_kernel(tc, z, credit, trust, h_words, h_sca
             for i, unit in enumerate(units):
                 coded[unit] = (codes, scales, i * UNIT)
 
-        todo = {(m, h): list(range(PASSES)) for m in range(E // M_TILE) for h in range(E // HALF)}
+        tiles_out = [(m, h) for j in range(E // UNIT) for h in range(E // HALF) for m in (2 * j, 2 * j + 1)]
+        todo = {tile_out: list(range(PASSES)) for tile_out in tiles_out}
         banks = {}
         free_banks = list(range(ACC_BANKS))
         closed = []
 
-        def ready(m, h, g):
-            left = ("L", g, m * M_TILE // UNIT) in coded
-            return left and (g >= FRESH or ("V", g, 2 * h) in coded)
-
         def multiply():
-            for h, m in [(h, m) for j in range(E // UNIT) for h in range(2) for m in (2 * j, 2 * j + 1)]:
-                now = [g for g in todo[(m, h)] if ready(m, h, g)]
-                if now and (m, h) not in banks and free_banks:
-                    b = free_banks.pop(0)
-                    banks[(m, h)] = (b, psum.tile([P, HALF], F32, name="acc", tag="acc%d" % b))
-                if not now or (m, h) not in banks:
+            for m, h in tiles_out:
+                j, m0 = divmod(m * M_TILE, UNIT)
+                ready = [g for g in todo[(m, h)] if ("L", g, j) in coded and (g >= FRESH or ("V", g, 2 * h) in coded)]
+                if ready and (m, h) not in banks and free_banks:
+                    bank = free_banks.pop(0)
+                    banks[(m, h)] = (bank, psum.tile([P, HALF], F32, name="acc", tag="acc%d" % bank))
+                if (m, h) not in banks:
                     continue
-                acc = banks[(m, h)][1]
-                for g in now:
+                for g in ready:
                     first = len(todo[(m, h)]) == PASSES
                     todo[(m, h)].remove(g)
                     last = not todo[(m, h)]
-                    codes, scales, c0 = coded[("L", g, m * M_TILE // UNIT)]
-                    c0 = c0 + (m * M_TILE) % UNIT
+                    l_codes, l_scales, l0 = coded[("L", g, j)]
+                    l_cols = slice(l0 + m0, l0 + m0 + M_TILE)
                     if g < FRESH:
-                        v_codes, v_scales, v0 = coded[("V", g, 2 * h)]
+                        v_codes, v_scales = coded[("V", g, 2 * h)][0:2]
                         rhs, rhs_scale = v_codes[:].bitcast(FP8X4), v_scales[:]
                     else:
-                        rhs = h_tiles[g - FRESH][:, 2 * HALF * h : 2 * HALF * (h + 1)].bitcast(FP4X4)
+                        rhs = h_codes[g - FRESH][:, 2 * HALF * h : 2 * HALF * (h + 1)].bitcast(FP4X4)
                         rhs_scale = h_plane[:, g - FRESH, HALF * h : HALF * (h + 1)]
                     nc.tensor.matmul_mx(
-                        out=acc[:],
-                        lhsT=codes[:, c0 : c0 + M_TILE].bitcast(FP8X4),
-                        lhsT_scale=scales[:, c0 : c0 + M_TILE],
+                        out=banks[(m, h)][1][:],
+                        lhsT=l_codes[:, l_cols].bitcast(FP8X4),
+                        lhsT_scale=l_scales[:, l_cols],
                         rhs=rhs,
                         rhs_scale=rhs_scale,
                         start=first,
@@ -205,44 +189,45 @@ def tile_router_gate_coactivation_s1_kernel(tc, z, credit, trust, h_words, h_sca
                     if last:
                         closed.append((m, h))
 
-        def drain(share):
-            for i, (m, h) in enumerate(list(closed)):
-                closed.remove((m, h))
-                b, acc = banks[(m, h)]
+        def drain(with_vector):
+            for i, (m, h) in enumerate(closed):
+                bank, acc = banks[(m, h)]
                 res = outp.tile([P, HALF], F32, name="res")
-                if share and i % 2 == 1:
+                if with_vector and i % 2 == 1:
                     nc.vector.tensor_copy(out=res[:], in_=acc[:])
                 else:
                     nc.scalar.copy(out=res[:], in_=acc[:])
                 nc.sync.dma_start(out=out[m * M_TILE : (m + 1) * M_TILE, h * HALF : (h + 1) * HALF], in_=res[:])
-                free_banks.append(b)
+                free_banks.append(bank)
+            closed.clear()
 
         for s, step in enumerate(steps):
             for later in steps[s : s + AHEAD + 1]:
                 for side, g, j in later:
                     if (g, j) not in gates:
                         sigmoid(g, j)
+
             pair = stage.tile([P, 2 * UNIT * PACK], BF16, name="pair", align_bytes=64)
-            weigh(nc.vector, w_psum, step[0], pair[:, 0 : UNIT * PACK], 0, UNIT)
+            first_unit, second_unit = pair[:, 0 : UNIT * PACK], pair[:, UNIT * PACK : 2 * UNIT * PACK]
+            weigh(nc.vector, w_psum, step[0], first_unit, 0, UNIT)
             if len(step) == 3:
                 single = stage.tile([P, UNIT * PACK], BF16, name="single", align_bytes=64, bufs=1)
                 weigh(nc.gpsimd, w_sbuf, step[2], single, 0, POOL_COLS)
                 weigh(nc.vector, w_psum, step[2], single, POOL_COLS, UNIT)
-            weigh(nc.vector, w_psum, step[1], pair[:, UNIT * PACK : 2 * UNIT * PACK], 0, UNIT)
-            if len(step) == 3:
+                weigh(nc.vector, w_psum, step[1], second_unit, 0, UNIT)
                 quantize(step[2:3], single[:], "single%d" % s)
                 drain(False)
                 multiply()
                 quantize(step[0:2], pair[:], "pair%d" % s)
             else:
-                quantize(step[0:1], pair[:, 0 : UNIT * PACK], "a%d" % s)
-                quantize(step[1:2], pair[:, UNIT * PACK : 2 * UNIT * PACK], "b%d" % s)
+                weigh(nc.vector, w_psum, step[1], second_unit, 0, UNIT)
+                quantize(step[0:1], first_unit, "a%d" % s)
+                quantize(step[1:2], second_unit, "b%d" % s)
+
             for side, g, j in step:
                 if last_use[(g, j)] == s and (g, j) in slot_of:
                     free_slots.append(slot_of.pop((g, j)))
             drain(False)
             multiply()
-        drain(True)
-        multiply()
         drain(True)
         assert not any(todo.values())

from contextlib import ExitStack

import concourse.mybir as mybir
from concourse.masks import make_identity

T, R, E = 1536, 2560, 1024
FLOPS = 2 * (T + R) * E * E

F32 = mybir.dt.float32
BF16 = mybir.dt.bfloat16
I32 = mybir.dt.int32
U32 = mybir.dt.uint32
U8 = mybir.dt.uint8
FP8X4 = mybir.dt.float8_e4m3fn_x4
FP4X4 = mybir.dt.float4_e2m1fn_x4
MULT = mybir.AluOpType.mult
SIGMOID = mybir.ActivationFunctionType.Sigmoid

P = 128
PACK = 4
K_PASS = P * PACK
FRESH = T // K_PASS
REPLAY = R // K_PASS
PASSES = FRESH + REPLAY
WEIGHT_ROWS = PASSES + FRESH
UNIT = 256
HALF = 512
M_TILE = 128
ACC_BANKS = 7
GATE_SLOTS = 18
AHEAD = 2
POOL_COLS = 232
OUT_BUFS = 4
H_FIRST = 2


def plan_steps():
    def right(g, h):
        return [("V", g, 2 * h), ("V", g, 2 * h + 1)]

    def fresh(j):
        return [("L", g, j) for g in range(FRESH)]

    def replay(j):
        return [("L", g, j) for g in range(FRESH, PASSES)]

    order = []
    for g in range(FRESH):
        order = order + right(g, 0) + [fresh(0)[g]]
    replay_01 = [unit for both in zip(replay(0), replay(1)) for unit in both]
    order = order + replay_01[:-1]
    rest_of_1 = replay_01[-1:] + fresh(1)
    for g in range(FRESH):
        order = order + right(g, 1) + [rest_of_1[g]]
    order = order + replay(2)[:2] + rest_of_1[FRESH:] + replay(2)[2:] + fresh(2)
    order = order + replay(3) + fresh(3)
    return [order[i : i + 3] for i in range(0, len(order), 3)]


def tile_router_gate_coactivation_s1_kernel(tc, z, credit, trust, h_words, h_scales, out):
    nc = tc.nc
    steps = plan_steps()

    with ExitStack() as ctx:
        keep = ctx.enter_context(tc.tile_pool(name="keep", bufs=1))
        stage = ctx.enter_context(tc.tile_pool(name="stage", bufs=2))
        outp = ctx.enter_context(tc.tile_pool(name="outp", bufs=OUT_BUFS))
        psum = ctx.enter_context(tc.psum_pool(name="psum", bufs=1))
        ctx.enter_context(tc.manual_schedule())

        w_rows = keep.tile([P, K_PASS], BF16, name="w_rows")
        nc.gpsimd.memset(w_rows[:], 0.0)

        logits = {}
        h_codes = {}

        def load_z(g, c0, width):
            zt = keep.tile([P, PACK, width], BF16, name="z_%d_%d" % (g, c0))
            rows = z[g * K_PASS : (g + 1) * K_PASS, c0 : c0 + width]
            nc.sync.dma_start(out=zt[:], in_=rows.rearrange("(p t) n -> p t n", t=PACK))
            for c in range(0, width, UNIT):
                logits[(g, (c0 + c) // UNIT)] = zt[:, :, c : c + UNIT]

        def load_h(g0, g1):
            ht = keep.tile([P, g1 - g0, 2 * E], U8, name="h_%d" % g0, align_bytes=64)
            nc.sync.dma_start(out=ht[:].bitcast(I32), in_=h_words[g0:g1].rearrange("g p w -> p g w").bitcast(I32))
            for g in range(g0, g1):
                h_codes[g] = ht[:, g - g0, :]

        ident = keep.tile([P, P], F32, name="ident")
        make_identity(nc, ident[:])
        h_plane = keep.tile([P, REPLAY, E], U8, name="h_plane", align_bytes=64)
        nc.gpsimd.memset(h_plane[:].bitcast(I32), 0)

        load_z(0, 0, UNIT)
        nc.sync.dma_start(out=w_rows[0:PASSES, :], in_=credit.rearrange("(g k) -> g k", k=K_PASS))
        trust_rows = trust.rearrange("(g k) -> g k", k=K_PASS)
        nc.sync.dma_start(out=w_rows[PASSES : PASSES + 2, :], in_=trust_rows[0:2])
        nc.sync.dma_start(out=w_rows[PASSES + 2 : WEIGHT_ROWS, :], in_=trust_rows[2:FRESH])
        load_z(0, UNIT, UNIT)
        for g in range(1, PASSES):
            load_z(g, 0, HALF)
        for quadrant in range(4):
            nc.sync.dma_start(
                out=h_plane[32 * quadrant : 32 * quadrant + 4].bitcast(I32),
                in_=h_scales[:, 4 * quadrant : 4 * quadrant + 4, :].rearrange("g r n -> r g n").bitcast(I32),
            )
        load_h(0, H_FIRST)
        load_z(0, HALF, HALF)
        load_h(H_FIRST, REPLAY)
        for g in range(1, PASSES):
            load_z(g, HALF, HALF)

        w_bank = psum.tile([P, P, 2], F32, name="w_bank")
        w_words = w_rows[:].bitcast(F32)
        for u in range(2):
            nc.tensor.transpose(w_bank[:, :, u], w_words[:, u : K_PASS // 2 : 2], ident[:])
        w_psum = w_bank[:].rearrange("p j u -> p (j u)").bitcast(BF16).rearrange("p (j t) -> p j t", t=PACK)
        w_sbuf = keep.tile([P, WEIGHT_ROWS, PACK], F32, name="w_sbuf")
        nc.vector.tensor_copy(out=w_sbuf[:], in_=w_psum[:, 0:WEIGHT_ROWS, :])

        last_use = {(g, j): s for s, step in enumerate(steps) for side, g, j in step}
        gates = {}
        free_slots = list(range(GATE_SLOTS))
        slot_of = {}

        def sigmoid(g, j):
            slot_of[(g, j)] = free_slots.pop(0)
            gt = keep.tile([P, PACK, UNIT], F32, name="gate", tag="gate%d" % slot_of[(g, j)])
            nc.scalar.activation(out=gt[:], in_=logits[(g, j)], func=SIGMOID)
            gates[(g, j)] = gt

        def weigh(engine, weights, unit, dst, c0, c1):
            side, g, j = unit
            row = g if side == "L" else PASSES + g
            engine.tensor_tensor(
                out=dst[:, PACK * c0 : PACK * c1].rearrange("p (c i t) -> p c t i", i=2, t=PACK),
                in0=gates[(g, j)][:, :, c0:c1].rearrange("p t (c i) -> p c t i", i=2),
                in1=weights[:, row, :].unsqueeze(1).unsqueeze(3).to_broadcast([P, (c1 - c0) // 2, PACK, 2]),
                op=MULT,
            )

        coded = {}

        def quantize(units, src, name):
            width = UNIT * len(units)
            codes = keep.tile([P, width], U32, name="codes_" + name, align_bytes=64)
            scales = keep.tile([P, width], U8, name="scales_" + name, align_bytes=64)
            nc.vector.quantize_mx(out=codes[:].bitcast(FP8X4), scales=scales[:], in_=src)
            for i, unit in enumerate(units):
                coded[unit] = (codes, scales, i * UNIT)

        tiles_out = [(m, h) for j in range(E // UNIT) for h in range(E // HALF) for m in (2 * j, 2 * j + 1)]
        todo = {tile_out: list(range(PASSES)) for tile_out in tiles_out}
        banks = {}
        free_banks = list(range(ACC_BANKS))
        closed = []

        def multiply():
            for m, h in tiles_out:
                j, m0 = divmod(m * M_TILE, UNIT)
                ready = [g for g in todo[(m, h)] if ("L", g, j) in coded and (g >= FRESH or ("V", g, 2 * h) in coded)]
                if ready and (m, h) not in banks and free_banks:
                    bank = free_banks.pop(0)
                    banks[(m, h)] = (bank, psum.tile([P, HALF], F32, name="acc", tag="acc%d" % bank))
                if (m, h) not in banks:
                    continue
                for g in ready:
                    first = len(todo[(m, h)]) == PASSES
                    todo[(m, h)].remove(g)
                    last = not todo[(m, h)]
                    l_codes, l_scales, l0 = coded[("L", g, j)]
                    l_cols = slice(l0 + m0, l0 + m0 + M_TILE)
                    if g < FRESH:
                        v_codes, v_scales = coded[("V", g, 2 * h)][0:2]
                        rhs, rhs_scale = v_codes[:].bitcast(FP8X4), v_scales[:]
                    else:
                        rhs = h_codes[g - FRESH][:, 2 * HALF * h : 2 * HALF * (h + 1)].bitcast(FP4X4)
                        rhs_scale = h_plane[:, g - FRESH, HALF * h : HALF * (h + 1)]
                    nc.tensor.matmul_mx(
                        out=banks[(m, h)][1][:],
                        lhsT=l_codes[:, l_cols].bitcast(FP8X4),
                        lhsT_scale=l_scales[:, l_cols],
                        rhs=rhs,
                        rhs_scale=rhs_scale,
                        start=first,
                        stop=last,
                    )
                    if last:
                        closed.append((m, h))

        def drain(with_vector):
            for i, (m, h) in enumerate(closed):
                bank, acc = banks[(m, h)]
                res = outp.tile([P, HALF], F32, name="res")
                if with_vector and i % 2 == 1:
                    nc.vector.tensor_copy(out=res[:], in_=acc[:])
                else:
                    nc.scalar.copy(out=res[:], in_=acc[:])
                nc.sync.dma_start(out=out[m * M_TILE : (m + 1) * M_TILE, h * HALF : (h + 1) * HALF], in_=res[:])
                free_banks.append(bank)
            closed.clear()

        for s, step in enumerate(steps):
            for later in steps[s : s + AHEAD + 1]:
                for side, g, j in later:
                    if (g, j) not in gates:
                        sigmoid(g, j)

            pair = stage.tile([P, 2 * UNIT * PACK], BF16, name="pair", align_bytes=64)
            first_unit, second_unit = pair[:, 0 : UNIT * PACK], pair[:, UNIT * PACK : 2 * UNIT * PACK]
            weigh(nc.vector, w_psum, step[0], first_unit, 0, UNIT)
            if len(step) == 3:
                single = stage.tile([P, UNIT * PACK], BF16, name="single", align_bytes=64, bufs=1)
                weigh(nc.gpsimd, w_sbuf, step[2], single, 0, POOL_COLS)
                weigh(nc.vector, w_psum, step[2], single, POOL_COLS, UNIT)
                weigh(nc.vector, w_psum, step[1], second_unit, 0, UNIT)
                quantize(step[2:3], single[:], "single%d" % s)
                drain(False)
                multiply()
                quantize(step[0:2], pair[:], "pair%d" % s)
            else:
                weigh(nc.vector, w_psum, step[1], second_unit, 0, UNIT)
                quantize(step[0:1], first_unit, "a%d" % s)
                quantize(step[1:2], second_unit, "b%d" % s)

            for side, g, j in step:
                if last_use[(g, j)] == s and (g, j) in slot_of:
                    free_slots.append(slot_of.pop((g, j)))
            drain(False)
            multiply()
        drain(True)
        assert not any(todo.values())
